import numpy as np
import ml_dtypes


def mxq(x, axis, fmt="e4m3"):
    dtype, down = {"e4m3": (ml_dtypes.float8_e4m3fn, 7), "e5m2": (ml_dtypes.float8_e5m2, 14)}[fmt]
    v = np.moveaxis(np.asarray(x, np.float32).astype(ml_dtypes.bfloat16).astype(np.float64), axis, -1)
    blocks = v.reshape(v.shape[:-1] + (-1, 32))
    amax = np.abs(blocks).max(-1, keepdims=True)
    byte = np.maximum(np.where(amax > 0, np.frexp(amax)[1] - 1 + 127, 0) - down, 1)
    scale = np.exp2(byte - 127.0)
    codes = (blocks / scale).astype(np.float32).astype(dtype).astype(np.float64)
    return np.moveaxis((codes * scale).reshape(v.shape), -1, axis)


WIDE = False


def mx_kscale(k, group=512):
    if not WIDE:
        return np.ones(k)
    levels = np.array([10, -10, 5, -5, 0])
    if group != 512:
        return np.exp2(np.random.permutation(np.resize(levels, k // group))).repeat(group)
    if k % 512:
        return np.exp2(np.random.permutation(np.resize(levels, k // 32))).repeat(32)
    a = np.empty((k // 512, 16))
    for p in range(k // 512):
        a[p, :8] = np.random.permutation(np.resize(levels, 8))
        for g in range(8):
            far = levels[np.abs(levels - a[p, g]) >= 10]
            a[p, g + 8] = far[np.random.randint(len(far))]
    return np.exp2(a.ravel()).repeat(32)


def f64(x):
    return np.asarray(x).astype(np.float64)


E2M1 = np.array([0.0, 0.5, 1.0, 1.5, 2.0, 3.0, 4.0, 6.0, -0.0, -0.5, -1.0, -1.5, -2.0, -3.0, -4.0, -6.0])


def pack_group(w):
    k, n = w.shape
    w = f64(np.asarray(w, np.float32).astype(ml_dtypes.bfloat16)).reshape(k // 32, 32, n)
    amax = np.abs(w).max(1)
    mant, ex = np.frexp(amax / 6.0)
    byte = np.clip(np.where(amax > 0, np.where(mant > 0.5, ex, ex - 1) + 127, 1), 1, 254)
    scaled = (w * np.exp2(127.0 - byte)[:, None, :]).reshape(k, n).astype(np.float32)
    c = np.ascontiguousarray(scaled.reshape(k // 4, 4, n).transpose(0, 2, 1)).astype(ml_dtypes.float4_e2m1fn).view(np.uint8) & 0xF
    return np.ascontiguousarray((c[..., 0::2] | (c[..., 1::2] << 4)).reshape(k // 4, 2 * n)), byte.astype(np.uint8)


def unpack_group(words, scales):
    p, n = words.shape[0], scales.shape[1]
    words = np.ascontiguousarray(words).reshape(p, n, 2)
    nib = np.empty((p, n, 4), np.uint8)
    nib[..., 0::2] = words & 0xF
    nib[..., 1::2] = words >> 4
    return E2M1[nib].transpose(0, 2, 1).reshape(4 * p, n) * np.repeat(np.exp2(scales.astype(np.float64) - 127.0), 32, axis=0)


G, D, M, N = 4, 256, 128, 1024


def setup_inputs():
    n = np.random.standard_normal
    s = mx_kscale(D, 0)[:, None]
    w_ = [pack_group(w) for w in n((G, D, M)) / np.sqrt(D) / s]
    u_ = [pack_group(w) for w in n((G, D, M)) / np.sqrt(D) / s]
    return {
        "x": (n((G, D, N)) * s).astype(np.float32),
        "w_words": np.stack([w[0] for w in w_]),
        "w_scales": np.stack([w[1] for w in w_]),
        "u_words": np.stack([w[0] for w in u_]),
        "u_scales": np.stack([w[1] for w in u_]),
    }


def reference(x, w_words, w_scales, u_words, u_scales):
    xq = mxq(f64(x), 1, "e4m3")
    h = np.stack([unpack_group(w_words[g], w_scales[g]) for g in range(G)]).transpose(0, 2, 1) @ xq
    g = np.stack([unpack_group(u_words[g], u_scales[g]) for g in range(G)]).transpose(0, 2, 1) @ xq
    y = np.maximum(h, 0.0) * g
    return y

@@ -1,0 +1,144 @@
+from contextlib import ExitStack
+
+import concourse.mybir as mybir
+
+G, D, M, N = 4, 256, 128, 1024
+FLOPS = 2 * 2 * G * D * M * N
+
+F32 = mybir.dt.float32
+BF16 = mybir.dt.bfloat16
+I32 = mybir.dt.int32
+U32 = mybir.dt.uint32
+U8 = mybir.dt.uint8
+FP8X4 = mybir.dt.float8_e4m3fn_x4
+FP4X4 = mybir.dt.float4_e2m1fn_x4
+ALU = mybir.AluOpType
+
+P = 128
+PACK = 4
+ROWS = D // PACK
+SIDE = P // ROWS
+PAIRS = G // SIDE
+NT = 512
+CHUNKS = [(q, h) for q in range(PAIRS) for h in range(N // NT)]
+VEC_COLS = [320, 320, 256, 256]
+
+
+def tile_rows_gglu_relu_kernel(tc, x, w_words, w_scales, u_words, u_scales, out):
+    nc = tc.nc
+    with ExitStack() as ctx:
+        keep = ctx.enter_context(tc.tile_pool(name="keep", bufs=1))
+        psum = ctx.enter_context(tc.psum_pool(name="psum", bufs=2))
+        ctx.enter_context(tc.manual_schedule())
+
+        raw = [keep.tile([P, PACK, NT], F32, name="raw%d" % k, align_bytes=64) for k in range(4)]
+        grouped = [keep.tile([P, PACK * NT], BF16, name="grouped%d" % k, align_bytes=64) for k in range(4)]
+        codes = [keep.tile([P, NT], U32, name="codes%d" % k, align_bytes=64) for k in range(4)]
+        xscale = [keep.tile([P, NT], U8, name="xscale%d" % k, align_bytes=64) for k in range(4)]
+        gate = [keep.tile([P, SIDE, NT], F32, name="gate%d" % k, align_bytes=64) for k in range(4)]
+        res = [keep.tile([P, SIDE, NT], F32, name="res%d" % k, align_bytes=64) for k in range(4)]
+        words = {s: keep.tile([P, PAIRS, 2 * M], U8, name="words_" + s, align_bytes=64) for s in "uw"}
+        scales = {s: keep.tile([P, PAIRS, M], U8, name="scales_" + s, align_bytes=64) for s in "uw"}
+        words_in = {"u": u_words, "w": w_words}
+        scales_in = {"u": u_scales, "w": w_scales}
+
+        x_rows = x.rearrange("(q c) (p j) n -> q (c p) j n", c=SIDE, j=PACK)
+
+        def load_x(k):
+            q, h = CHUNKS[k]
+            nc.sync.dma_start(out=raw[k][:], in_=x_rows[q, :, :, h * NT : (h + 1) * NT])
+
+        def load_words(s):
+            src = words_in[s].bitcast(I32).rearrange("(q c) p b -> (c p) q b", c=SIDE)
+            nc.scalar.dma_start(out=words[s][:].bitcast(I32), in_=src)
+
+        def load_scales(s, quad):
+            src = scales_in[s].bitcast(I32).rearrange("(q c) (f i) m -> (c f) i q m", c=SIDE, i=4)
+            (nc.scalar if s == "u" else nc.gpsimd).dma_start(out=scales[s][32 * quad : 32 * quad + 4].bitcast(I32), in_=src[quad])
+
+        def interleave(k, copy, a, b):
+            dst = grouped[k][:, PACK * a : PACK * b].rearrange("p (c i t) -> p c t i", i=4, t=PACK)
+            src = raw[k][:, :, a:b].rearrange("p t (c i) -> p c t i", i=4)
+            copy(out=dst, in_=src)
+
+        def copy_v(k):
+            interleave(k, nc.vector.tensor_copy, 0, VEC_COLS[k])
+
+        def copy_s(k):
+            interleave(k, nc.scalar.copy, VEC_COLS[k], NT)
+
+        def quantize(k):
+            nc.vector.quantize_mx(out=codes[k][:].bitcast(FP8X4), scales=xscale[k][:], in_=grouped[k][:])
+
+        acc = {}
+
+        def products(k):
+            q = CHUNKS[k][0]
+            for s in "uw":
+                for c in range(SIDE):
+                    rows = slice(ROWS * c, ROWS * (c + 1))
+                    acc[k, s, c] = psum.tile([M, NT], F32, name="acc_%s%d" % (s, c))
+                    nc.tensor.matmul_mx(
+                        out=acc[k, s, c][:],
+                        lhsT=words[s][rows, q, :].bitcast(FP4X4),
+                        lhsT_scale=scales[s][rows, q, :],
+                        rhs=codes[k][rows, :].bitcast(FP8X4),
+                        rhs_scale=xscale[k][rows, :],
+                        start=True,
+                        stop=True,
+                    )
+
+        def evac(k, c):
+            nc.scalar.copy(out=gate[k][:, c, :], in_=acc[k, "u", c][:])
+
+        def finish(k, c):
+            nc.vector.scalar_tensor_tensor(
+                out=res[k][:, c, :], in0=acc[k, "w", c][:], scalar=0.0, in1=gate[k][:, c, :], op0=ALU.max, op1=ALU.mult
+            )
+
+        def store(k, cs):
+            q, h = CHUNKS[k]
+            dst = out[SIDE * q + cs.start : SIDE * q + cs.stop, :, h * NT : (h + 1) * NT].rearrange("c m n -> m c n")
+            nc.sync.dma_start(out=dst, in_=res[k][:, cs, :])
+
+        nc.vector.memset(scales["u"][:].bitcast(I32), 0)
+        nc.gpsimd.memset(scales["w"][:].bitcast(I32), 0)
+
+        load_x(0)
+        load_words("u")
+        load_x(1)
+        load_words("w")
+        for quad in range(4):
+            load_scales("u", quad)
+            load_scales("w", quad)
+        load_x(2)
+        load_x(3)
+
+        copy_v(0)
+        copy_s(0)
+        quantize(0)
+        products(0)
+        copy_v(1)
+        copy_s(1)
+        quantize(1)
+        products(1)
+        evac(0, 0)
+        evac(0, 1)
+        finish(0, 0)
+        for k in range(2, 4):
+            copy_v(k)
+            copy_s(k)
+            finish(k - 2, 1)
+            quantize(k)
+            products(k)
+            store(k - 2, slice(0, 2) if k == 2 else slice(1, 2))
+            evac(k - 1, 0)
+            evac(k - 1, 1)
+            finish(k - 1, 0)
+            store(k - 1, slice(0, 1))
+        finish(2, 1)
+        store(2, slice(1, 2))
+        for c in range(2):
+            evac(3, c)
+            finish(3, c)
+            store(3, slice(c, c + 1))

@@ -50,11 +50,11 @@ def tile_rows_gglu_relu_kernel(tc, x, w_words, w_scales, u_words, u_scales, out)
 
         def load_words(s):
             src = words_in[s].bitcast(I32).rearrange("(q c) p b -> (c p) q b", c=SIDE)
-            nc.scalar.dma_start(out=words[s][:].bitcast(I32), in_=src)
+            nc.sync.dma_start(out=words[s][:].bitcast(I32), in_=src)
 
         def load_scales(s, quad):
             src = scales_in[s].bitcast(I32).rearrange("(q c) (f i) m -> (c f) i q m", c=SIDE, i=4)
-            (nc.scalar if s == "u" else nc.gpsimd).dma_start(out=scales[s][32 * quad : 32 * quad + 4].bitcast(I32), in_=src[quad])
+            nc.sync.dma_start(out=scales[s][32 * quad : 32 * quad + 4].bitcast(I32), in_=src[quad])
 
         def interleave(k, copy, a, b):
             dst = grouped[k][:, PACK * a : PACK * b].rearrange("p (c i t) -> p c t i", i=4, t=PACK)
@@ -101,15 +101,17 @@ def tile_rows_gglu_relu_kernel(tc, x, w_words, w_scales, u_words, u_scales, out)
             dst = out[SIDE * q + cs.start : SIDE * q + cs.stop, :, h * NT : (h + 1) * NT].rearrange("c m n -> m c n")
             nc.sync.dma_start(out=dst, in_=res[k][:, cs, :])
 
-        nc.vector.memset(scales["u"][:].bitcast(I32), 0)
-        nc.gpsimd.memset(scales["w"][:].bitcast(I32), 0)
+        for s in "uw":
+            nc.vector.memset(scales[s][:].bitcast(I32), 0)
 
-        load_x(0)
         load_words("u")
-        load_x(1)
-        load_words("w")
+        load_x(0)
         for quad in range(4):
             load_scales("u", quad)
+        load_words("w")
+        load_scales("w", 0)
+        load_x(1)
+        for quad in range(1, 4):
             load_scales("w", quad)
         load_x(2)
         load_x(3)

@@ -21,7 +21,8 @@ SIDE = P // ROWS
 PAIRS = G // SIDE
 NT = 512
 CHUNKS = [(q, h) for q in range(PAIRS) for h in range(N // NT)]
-VEC_COLS = [320, 320, 256, 256]
+PIECES = [[(0, 512)], [(0, 512)], [(0, 512)], [(0, 256), (256, 512)]]
+VEC_COLS = [[320], [320], [320], [0, 160]]
 
 
 def tile_rows_gglu_relu_kernel(tc, x, w_words, w_scales, u_words, u_scales, out):
@@ -31,7 +32,11 @@ def tile_rows_gglu_relu_kernel(tc, x, w_words, w_scales, u_words, u_scales, out)
         psum = ctx.enter_context(tc.psum_pool(name="psum", bufs=2))
         ctx.enter_context(tc.manual_schedule())
 
-        raw = [keep.tile([P, PACK, NT], F32, name="raw%d" % k, align_bytes=64) for k in range(4)]
+        raw = {
+            (k, a): keep.tile([P, PACK, b - a], F32, name="raw%d_%d" % (k, a), align_bytes=64)
+            for k in range(4)
+            for a, b in PIECES[k]
+        }
         grouped = [keep.tile([P, PACK * NT], BF16, name="grouped%d" % k, align_bytes=64) for k in range(4)]
         codes = [keep.tile([P, NT], U32, name="codes%d" % k, align_bytes=64) for k in range(4)]
         xscale = [keep.tile([P, NT], U8, name="xscale%d" % k, align_bytes=64) for k in range(4)]
@@ -44,9 +49,10 @@ def tile_rows_gglu_relu_kernel(tc, x, w_words, w_scales, u_words, u_scales, out)
 
         x_rows = x.rearrange("(q c) (p j) n -> q (c p) j n", c=SIDE, j=PACK)
 
-        def load_x(k):
+        def load_x(k, j=0):
             q, h = CHUNKS[k]
-            nc.sync.dma_start(out=raw[k][:], in_=x_rows[q, :, :, h * NT : (h + 1) * NT])
+            a, b = PIECES[k][j]
+            nc.sync.dma_start(out=raw[k, a][:], in_=x_rows[q, :, :, h * NT + a : h * NT + b])
 
         def load_words(s):
             src = words_in[s].bitcast(I32).rearrange("(q c) p b -> (c p) q b", c=SIDE)
@@ -56,19 +62,24 @@ def tile_rows_gglu_relu_kernel(tc, x, w_words, w_scales, u_words, u_scales, out)
             src = scales_in[s].bitcast(I32).rearrange("(q c) (f i) m -> (c f) i q m", c=SIDE, i=4)
             nc.sync.dma_start(out=scales[s][32 * quad : 32 * quad + 4].bitcast(I32), in_=src[quad])
 
-        def interleave(k, copy, a, b):
-            dst = grouped[k][:, PACK * a : PACK * b].rearrange("p (c i t) -> p c t i", i=4, t=PACK)
-            src = raw[k][:, :, a:b].rearrange("p t (c i) -> p c t i", i=4)
+        def interleave(k, j, copy, lo, hi):
+            a = PIECES[k][j][0]
+            dst = grouped[k][:, PACK * (a + lo) : PACK * (a + hi)].rearrange("p (c i t) -> p c t i", i=4, t=PACK)
+            src = raw[k, a][:, :, lo:hi].rearrange("p t (c i) -> p c t i", i=4)
             copy(out=dst, in_=src)
 
-        def copy_v(k):
-            interleave(k, nc.vector.tensor_copy, 0, VEC_COLS[k])
+        def copy_v(k, j=0):
+            interleave(k, j, nc.vector.tensor_copy, 0, VEC_COLS[k][j])
 
-        def copy_s(k):
-            interleave(k, nc.scalar.copy, VEC_COLS[k], NT)
+        def copy_s(k, j=0):
+            a, b = PIECES[k][j]
+            interleave(k, j, nc.scalar.copy, VEC_COLS[k][j], b - a)
 
-        def quantize(k):
-            nc.vector.quantize_mx(out=codes[k][:].bitcast(FP8X4), scales=xscale[k][:], in_=grouped[k][:])
+        def quantize(k, j=0):
+            a, b = PIECES[k][j]
+            nc.vector.quantize_mx(
+                out=codes[k][:, a:b].bitcast(FP8X4), scales=xscale[k][:, a:b], in_=grouped[k][:, PACK * a : PACK * b]
+            )
 
         acc = {}
 
@@ -88,59 +99,71 @@ def tile_rows_gglu_relu_kernel(tc, x, w_words, w_scales, u_words, u_scales, out)
                         stop=True,
                     )
 
-        def evac(k, c):
-            nc.scalar.copy(out=gate[k][:, c, :], in_=acc[k, "u", c][:])
+        def evac(k, c, a=0, b=NT):
+            nc.scalar.copy(out=gate[k][:, c, a:b], in_=acc[k, "u", c][:, a:b])
 
-        def finish(k, c):
+        def finish(k, c, a=0, b=NT):
             nc.vector.scalar_tensor_tensor(
-                out=res[k][:, c, :], in0=acc[k, "w", c][:], scalar=0.0, in1=gate[k][:, c, :], op0=ALU.max, op1=ALU.mult
+                out=res[k][:, c, a:b],
+                in0=acc[k, "w", c][:, a:b],
+                scalar=0.0,
+                in1=gate[k][:, c, a:b],
+                op0=ALU.max,
+                op1=ALU.mult,
             )
 
-        def store(k, cs):
+        def store(k, cs, a=0, b=NT):
             q, h = CHUNKS[k]
-            dst = out[SIDE * q + cs.start : SIDE * q + cs.stop, :, h * NT : (h + 1) * NT].rearrange("c m n -> m c n")
-            nc.sync.dma_start(out=dst, in_=res[k][:, cs, :])
+            dst = out[SIDE * q + cs.start : SIDE * q + cs.stop, :, h * NT + a : h * NT + b].rearrange("c m n -> m c n")
+            nc.sync.dma_start(out=dst, in_=res[k][:, cs, a:b])
 
         for s in "uw":
             nc.vector.memset(scales[s][:].bitcast(I32), 0)
 
-        load_words("u")
         load_x(0)
+        load_words("u")
         for quad in range(4):
             load_scales("u", quad)
         load_words("w")
-        load_scales("w", 0)
         load_x(1)
-        for quad in range(1, 4):
+        for quad in range(4):
             load_scales("w", quad)
         load_x(2)
-        load_x(3)
+        for j in range(len(PIECES[3])):
+            load_x(3, j)
 
-        copy_v(0)
-        copy_s(0)
-        quantize(0)
-        products(0)
-        copy_v(1)
-        copy_s(1)
-        quantize(1)
-        products(1)
+        for k in range(2):
+            copy_v(k)
+            copy_s(k)
+            quantize(k)
+            products(k)
         evac(0, 0)
         evac(0, 1)
         finish(0, 0)
-        for k in range(2, 4):
-            copy_v(k)
-            copy_s(k)
-            finish(k - 2, 1)
-            quantize(k)
-            products(k)
-            store(k - 2, slice(0, 2) if k == 2 else slice(1, 2))
-            evac(k - 1, 0)
-            evac(k - 1, 1)
-            finish(k - 1, 0)
-            store(k - 1, slice(0, 1))
-        finish(2, 1)
-        store(2, slice(1, 2))
+        copy_v(2)
+        copy_s(2)
+        finish(0, 1)
+        store(0, slice(0, 2))
+        quantize(2)
+        products(2)
         for c in range(2):
-            evac(3, c)
-            finish(3, c)
-            store(3, slice(c, c + 1))
+            evac(1, c)
+            finish(1, c)
+            store(1, slice(c, c + 1))
+        copy_s(3, 0)
+        copy_v(3, 1)
+        copy_s(3, 1)
+        quantize(3, 0)
+        quantize(3, 1)
+        products(3)
+        for c in range(2):
+            evac(2, c)
+            finish(2, c)
+            store(2, slice(c, c + 1))
+        evac(3, 0)
+        finish(3, 0)
+        store(3, slice(0, 1))
+        for a in (0, 256):
+            evac(3, 1, a, a + 256)
+            finish(3, 1, a, a + 256)
+            store(3, slice(1, 2), a, a + 256)

from contextlib import ExitStack

import concourse.mybir as mybir

G, D, M, N = 4, 256, 128, 1024
FLOPS = 2 * 2 * G * D * M * N

F32 = mybir.dt.float32
BF16 = mybir.dt.bfloat16
I32 = mybir.dt.int32
U32 = mybir.dt.uint32
U8 = mybir.dt.uint8
FP8X4 = mybir.dt.float8_e4m3fn_x4
FP4X4 = mybir.dt.float4_e2m1fn_x4
ALU = mybir.AluOpType

P = 128
PACK = 4
ROWS = D // PACK
SIDE = P // ROWS
PAIRS = G // SIDE
NT = 512
CHUNKS = [(q, h) for q in range(PAIRS) for h in range(N // NT)]
PIECES = [[(0, 512)], [(0, 512)], [(0, 512)], [(0, 256), (256, 512)]]
VEC_COLS = [[320], [320], [320], [0, 160]]


def tile_rows_gglu_relu_kernel(tc, x, w_words, w_scales, u_words, u_scales, out):
    nc = tc.nc
    with ExitStack() as ctx:
        keep = ctx.enter_context(tc.tile_pool(name="keep", bufs=1))
        psum = ctx.enter_context(tc.psum_pool(name="psum", bufs=2))
        ctx.enter_context(tc.manual_schedule())

        raw = {
            (k, a): keep.tile([P, PACK, b - a], F32, name="raw%d_%d" % (k, a), align_bytes=64)
            for k in range(4)
            for a, b in PIECES[k]
        }
        grouped = [keep.tile([P, PACK * NT], BF16, name="grouped%d" % k, align_bytes=64) for k in range(4)]
        codes = [keep.tile([P, NT], U32, name="codes%d" % k, align_bytes=64) for k in range(4)]
        xscale = [keep.tile([P, NT], U8, name="xscale%d" % k, align_bytes=64) for k in range(4)]
        gate = [keep.tile([P, SIDE, NT], F32, name="gate%d" % k, align_bytes=64) for k in range(4)]
        res = [keep.tile([P, SIDE, NT], F32, name="res%d" % k, align_bytes=64) for k in range(4)]
        words = {s: keep.tile([P, PAIRS, 2 * M], U8, name="words_" + s, align_bytes=64) for s in "uw"}
        scales = {s: keep.tile([P, PAIRS, M], U8, name="scales_" + s, align_bytes=64) for s in "uw"}
        words_in = {"u": u_words, "w": w_words}
        scales_in = {"u": u_scales, "w": w_scales}

        x_rows = x.rearrange("(q c) (p j) n -> q (c p) j n", c=SIDE, j=PACK)

        def load_x(k, j=0):
            q, h = CHUNKS[k]
            a, b = PIECES[k][j]
            nc.sync.dma_start(out=raw[k, a][:], in_=x_rows[q, :, :, h * NT + a : h * NT + b])

        def load_words(s):
            src = words_in[s].bitcast(I32).rearrange("(q c) p b -> (c p) q b", c=SIDE)
            nc.sync.dma_start(out=words[s][:].bitcast(I32), in_=src)

        def load_scales(s, quad):
            src = scales_in[s].bitcast(I32).rearrange("(q c) (f i) m -> (c f) i q m", c=SIDE, i=4)
            nc.sync.dma_start(out=scales[s][32 * quad : 32 * quad + 4].bitcast(I32), in_=src[quad])

        def interleave(k, j, copy, lo, hi):
            a = PIECES[k][j][0]
            dst = grouped[k][:, PACK * (a + lo) : PACK * (a + hi)].rearrange("p (c i t) -> p c t i", i=4, t=PACK)
            src = raw[k, a][:, :, lo:hi].rearrange("p t (c i) -> p c t i", i=4)
            copy(out=dst, in_=src)

        def copy_v(k, j=0):
            interleave(k, j, nc.vector.tensor_copy, 0, VEC_COLS[k][j])

        def copy_s(k, j=0):
            a, b = PIECES[k][j]
            interleave(k, j, nc.scalar.copy, VEC_COLS[k][j], b - a)

        def quantize(k, j=0):
            a, b = PIECES[k][j]
            nc.vector.quantize_mx(
                out=codes[k][:, a:b].bitcast(FP8X4), scales=xscale[k][:, a:b], in_=grouped[k][:, PACK * a : PACK * b]
            )

        acc = {}

        def products(k):
            q = CHUNKS[k][0]
            for s in "uw":
                for c in range(SIDE):
                    rows = slice(ROWS * c, ROWS * (c + 1))
                    acc[k, s, c] = psum.tile([M, NT], F32, name="acc_%s%d" % (s, c))
                    nc.tensor.matmul_mx(
                        out=acc[k, s, c][:],
                        lhsT=words[s][rows, q, :].bitcast(FP4X4),
                        lhsT_scale=scales[s][rows, q, :],
                        rhs=codes[k][rows, :].bitcast(FP8X4),
                        rhs_scale=xscale[k][rows, :],
                        start=True,
                        stop=True,
                    )

        def evac(k, c, a=0, b=NT):
            nc.scalar.copy(out=gate[k][:, c, a:b], in_=acc[k, "u", c][:, a:b])

        def finish(k, c, a=0, b=NT):
            nc.vector.scalar_tensor_tensor(
                out=res[k][:, c, a:b],
                in0=acc[k, "w", c][:, a:b],
                scalar=0.0,
                in1=gate[k][:, c, a:b],
                op0=ALU.max,
                op1=ALU.mult,
            )

        def store(k, cs, a=0, b=NT):
            q, h = CHUNKS[k]
            dst = out[SIDE * q + cs.start : SIDE * q + cs.stop, :, h * NT + a : h * NT + b].rearrange("c m n -> m c n")
            nc.sync.dma_start(out=dst, in_=res[k][:, cs, a:b])

        for s in "uw":
            nc.vector.memset(scales[s][:].bitcast(I32), 0)

        load_x(0)
        load_words("u")
        for quad in range(4):
            load_scales("u", quad)
        load_words("w")
        load_x(1)
        for quad in range(4):
            load_scales("w", quad)
        load_x(2)
        for j in range(len(PIECES[3])):
            load_x(3, j)

        for k in range(2):
            copy_v(k)
            copy_s(k)
            quantize(k)
            products(k)
        evac(0, 0)
        evac(0, 1)
        finish(0, 0)
        copy_v(2)
        copy_s(2)
        finish(0, 1)
        store(0, slice(0, 2))
        quantize(2)
        products(2)
        for c in range(2):
            evac(1, c)
            finish(1, c)
            store(1, slice(c, c + 1))
        copy_s(3, 0)
        copy_v(3, 1)
        copy_s(3, 1)
        quantize(3, 0)
        quantize(3, 1)
        products(3)
        for c in range(2):
            evac(2, c)
            finish(2, c)
            store(2, slice(c, c + 1))
        evac(3, 0)
        finish(3, 0)
        store(3, slice(0, 1))
        for a in (0, 256):
            evac(3, 1, a, a + 256)
            finish(3, 1, a, a + 256)
            store(3, slice(1, 2), a, a + 256)
